import numpy as np
import ml_dtypes


def mxq(x, axis, fmt="e4m3"):
    dtype, down = {"e4m3": (ml_dtypes.float8_e4m3fn, 7), "e5m2": (ml_dtypes.float8_e5m2, 14)}[fmt]
    v = np.moveaxis(np.asarray(x, np.float32).astype(ml_dtypes.bfloat16).astype(np.float64), axis, -1)
    blocks = v.reshape(v.shape[:-1] + (-1, 32))
    amax = np.abs(blocks).max(-1, keepdims=True)
    byte = np.maximum(np.where(amax > 0, np.frexp(amax)[1] - 1 + 127, 0) - down, 1)
    scale = np.exp2(byte - 127.0)
    codes = (blocks / scale).astype(np.float32).astype(dtype).astype(np.float64)
    return np.moveaxis((codes * scale).reshape(v.shape), -1, axis)


WIDE = False


def mx_kscale(k):
    if not WIDE:
        return np.ones(k)
    levels = np.array([10, -10, 5, -5, 0])
    if k % 512:
        return np.exp2(np.random.permutation(np.resize(levels, k // 32))).repeat(32)
    a = np.empty((k // 512, 16))
    for p in range(k // 512):
        a[p, :8] = np.random.permutation(np.resize(levels, 8))
        for g in range(8):
            far = levels[np.abs(levels - a[p, g]) >= 10]
            a[p, g + 8] = far[np.random.randint(len(far))]
    return np.exp2(a.ravel()).repeat(32)


def f64(x):
    return np.asarray(x).astype(np.float64)


def striped(idx):
    return np.tile(idx.reshape(-1, 16).T, (8, 1)).astype(np.uint16)


def unstriped(offs):
    return offs[:16].T.reshape(-1).astype(np.int64)


E2M1 = np.array([0.0, 0.5, 1.0, 1.5, 2.0, 3.0, 4.0, 6.0, -0.0, -0.5, -1.0, -1.5, -2.0, -3.0, -4.0, -6.0])


def pack_weight(w, fmt):
    k, n = w.shape
    w = f64(np.asarray(w, np.float32).astype(ml_dtypes.bfloat16)).reshape(k // 32, 32, n)
    amax = np.abs(w).max(1)
    if fmt == "e4m3":
        byte = np.frexp(amax)[1] - 1 + 127 - 7
    else:
        mant, ex = np.frexp(amax / 6.0)
        byte = np.where(mant > 0.5, ex, ex - 1) + 127
    byte = np.clip(np.where(amax > 0, byte, 1), 1, 254)
    scaled = (w * np.exp2(127.0 - byte)[:, None, :]).reshape(k, n).astype(np.float32)
    by_word = np.ascontiguousarray(scaled.reshape(k // 512, 128, 4, n).transpose(0, 1, 3, 2))
    if fmt == "e4m3":
        words = by_word.astype(ml_dtypes.float8_e4m3fn).view(np.uint8)
    else:
        c = by_word.astype(ml_dtypes.float4_e2m1fn).view(np.uint8) & 0xF
        words = (c[..., 0::2] | (c[..., 1::2] << 4)).reshape(k // 512, 128, 2 * n)
    return np.ascontiguousarray(words), np.ascontiguousarray(byte.astype(np.uint8).reshape(k // 512, 16, n))


def unpack_weight(words, scales, fmt):
    g, _, n = scales.shape
    words = np.ascontiguousarray(words).reshape(g, 128, n, -1)
    if fmt == "e4m3":
        vals = words.view(ml_dtypes.float8_e4m3fn).astype(np.float64)
    else:
        nib = np.empty((g, 128, n, 4), np.uint8)
        nib[..., 0::2] = words & 0xF
        nib[..., 1::2] = words >> 4
        vals = E2M1[nib]
    vals = vals * np.repeat(np.exp2(scales.astype(np.float64) - 127.0), 8, axis=1)[..., None]
    return vals.transpose(0, 1, 3, 2).reshape(g * 512, n)


def relu(v):
    return np.maximum(v, 0.0)


K, T, E, C, H, N = 1536, 768, 2, 256, 512, 128


def by_expert(wq, xq):
    return np.concatenate([wq[e].T @ xq[:, e * C:(e + 1) * C] for e in range(E)], axis=1)


def setup_inputs():
    n = np.random.standard_normal
    s = mx_kscale(K)[:, None]
    u = mx_kscale(H)
    w1 = [pack_weight(m, "e2m1") for m in n((E + 1, K, H)) / np.sqrt(K) / s[None] * u[None, None, :]]
    w2 = [pack_weight(m, "e2m1") for m in n((E + 1, H, N)) / np.sqrt(H) / u[None, :, None]]
    return {
        "xT": (n((K, T)) * s).astype(np.float32),
        "w1_words": np.stack([m[0] for m in w1]),
        "w1_scales": np.stack([m[1] for m in w1]),
        "w2_words": np.stack([m[0] for m in w2]),
        "w2_scales": np.stack([m[1] for m in w2]),
        "gate": np.tile(np.random.uniform(0.2, 1.0, E * C), (N, 1)).astype(np.float32),
        "offs": striped(np.random.permutation(T)[:E * C]),
    }


def reference(xT, w1_words, w1_scales, w2_words, w2_scales, gate, offs):
    idx = unstriped(offs)
    w1 = np.stack([unpack_weight(w1_words[e], w1_scales[e], "e2m1") for e in range(E + 1)])
    w2 = np.stack([unpack_weight(w2_words[e], w2_scales[e], "e2m1") for e in range(E + 1)])
    w1q, w2q = w1, w2
    xs = mxq(f64(xT), 0, "e4m3")
    hs = relu(w1q[E].T @ xs)
    ys = w2q[E].T @ mxq(hs, 0, "e4m3")
    xq = mxq(f64(xT)[:, idx], 0, "e4m3")
    h = relu(by_expert(w1q, xq))
    y = by_expert(w2q, mxq(h, 0, "e4m3"))
    out = ys
    out[:, idx] += f64(gate) * y
    return out

@@ -1,0 +1,264 @@
+from contextlib import ExitStack
+
+import concourse.mybir as mybir
+from concourse.masks import make_identity
+
+K, T, E, C, H, N = 1536, 768, 2, 256, 512, 128
+P = 128
+S = E * C
+PASSES = K // 512
+TA = 256
+FLOPS = 2 * (S + T) * (K * H + H * N)
+
+F32 = mybir.dt.float32
+BF16 = mybir.dt.bfloat16
+I32 = mybir.dt.int32
+U32 = mybir.dt.uint32
+U16 = mybir.dt.uint16
+U8 = mybir.dt.uint8
+FP8X4 = mybir.dt.float8_e4m3fn_x4
+FP4X4 = mybir.dt.float4_e2m1fn_x4
+RELU = mybir.ActivationFunctionType.Relu
+COPY = mybir.ActivationFunctionType.Copy
+MULT = mybir.AluOpType.mult
+ADD = mybir.AluOpType.add
+
+
+def tile_moe_shr_mlp_relu_kernel(tc, xT, w1_words, w1_scales, w2_words, w2_scales, gate, offs, out):
+    nc = tc.nc
+    with ExitStack() as ctx:
+        keep = ctx.enter_context(tc.tile_pool(name="keep", bufs=1))
+        ring = ctx.enter_context(tc.tile_pool(name="ring", bufs=4))
+        psum = ctx.enter_context(tc.psum_pool(name="psum", bufs=1))
+
+        xraw = {}
+        w1w = {}
+        offsets = keep.tile([P, S // 16], U16, name="offsets")
+        w1s = keep.tile([P, (E + 1) * PASSES, H], U8, align_bytes=64, name="w1s")
+        w2s = keep.tile([P, E + 1, N], U8, align_bytes=64, name="w2s")
+        w2w = keep.tile([P, E + 1, 2 * N], U8, align_bytes=64, name="w2w")
+        gate_sb = keep.tile([P, S], F32, name="gate_sb")
+        for s in range(PASSES):
+            xraw[s] = keep.tile([P, 4, T], F32, name=f"xraw{s}")
+            w1w[s] = keep.tile([P, E + 1, 2 * H], U8, align_bytes=64, name=f"w1w{s}")
+
+        def load_x(s, u, a, b):
+            src = xT[512 * s:512 * (s + 1), :].rearrange("(p j) t -> p j t", j=4)
+            rows = slice(0, 4) if u is None else slice(2 * u, 2 * u + 2)
+            nc.sync.dma_start(xraw[s][:, rows, a:b], src[:, rows, a:b])
+
+        def load_w1(s, e0, e1):
+            nc.sync.dma_start(
+                w1w[s][:, e0:e1].rearrange("p e b -> p (e b)").bitcast(I32).rearrange("p (e b) -> p e b", e=e1 - e0),
+                w1_words.bitcast(I32)[e0:e1, s].rearrange("e p b -> p e b"),
+            )
+
+        warm = keep.tile([P, 1], F32, name="warm")
+        nc.vector.memset(warm[:], 0.0)
+        nc.scalar.activation(warm[:], warm[:], RELU)
+
+        w1s_i = w1s[:].rearrange("p a i -> p (a i)").bitcast(I32)
+        w2s_i = w2s[:].rearrange("p a i -> p (a i)").bitcast(I32)
+        nc.vector.memset(w1s_i, 0)
+        nc.gpsimd.memset(w2s_i, 0)
+        w1s_i = w1s_i.rearrange("p (a i) -> p a i", i=H // 4)
+        w2s_i = w2s_i.rearrange("p (a i) -> p a i", i=N // 4)
+
+
+        def load_scales1():
+            for q in range(4):
+                nc.scalar.dma_start(
+                    w1s_i[32 * q:32 * q + 4],
+                    w1_scales.bitcast(I32)[:, :, 4 * q:4 * q + 4, :].rearrange("e s q i -> q (e s) i"),
+                )
+
+        def load_scales2():
+            for q in range(4):
+                nc.sync.dma_start(
+                    w2s_i[32 * q:32 * q + 4],
+                    w2_scales.bitcast(I32)[:, 0, 4 * q:4 * q + 4, :].rearrange("e q i -> q e i"),
+                )
+
+        def load_w2():
+            nc.sync.dma_start(
+                w2w[:].rearrange("p e b -> p (e b)").bitcast(I32).rearrange("p (e b) -> p e b", e=E + 1),
+                w2_words.bitcast(I32)[:, 0].rearrange("e p b -> p e b"),
+            )
+
+        load_x(0, 0, 0, TA)
+        load_x(0, 1, 0, TA)
+        load_scales1()
+        load_w1(0, E, E + 1)
+        nc.sync.dma_start(offsets[:], offs)
+        for s in (1, 2):
+            load_x(s, None, 0, TA)
+            load_w1(s, E, E + 1)
+        for s in range(PASSES):
+            load_x(s, 0, TA, T)
+            load_x(s, 1, TA, T)
+            load_w1(s, 0, E)
+            if s == 0:
+                load_w2()
+                load_scales2()
+        nc.sync.dma_start(gate_sb[:], gate)
+
+        ident = keep.tile([P, P], F32, name="ident")
+        make_identity(nc, ident[:])
+        scat = keep.tile([P, T], F32, name="scat")
+        nc.gpsimd.memset(scat[:], 0.0)
+
+        acc = {}
+        codes = {}
+        pw = {}
+        sg = {}
+        tq = {}
+        for s in range(PASSES):
+            pw[s] = keep.tile([P, 2, T, 2], BF16, align_bytes=64, name=f"pw{s}")
+            sg[s] = keep.tile([P, S, 4], BF16, align_bytes=64, name=f"sg{s}")
+            tq[s] = keep.tile([P, T, 4], BF16, align_bytes=64, name=f"tq{s}")
+            c = keep.tile([P, T], U32, align_bytes=64, name=f"tc{s}")
+            sc = keep.tile([P, T], U8, align_bytes=64, name=f"ts{s}")
+            codes["tok", s] = (c, sc)
+            c = keep.tile([P, S], U32, align_bytes=64, name=f"sc{s}")
+            sc = keep.tile([P, S], U8, align_bytes=64, name=f"ss{s}")
+            codes["slot", s] = (c, sc)
+
+        def cast(eng, s, u, a, b):
+            o = pw[s][:, u, a:b, :]
+            i = xraw[s][:, 2 * u:2 * u + 2, a:b].rearrange("p j t -> p t j")
+            if eng == "v":
+                nc.vector.tensor_copy(o, i)
+            elif eng == "s":
+                nc.scalar.copy(o, i)
+            else:
+                nc.gpsimd.tensor_scalar(o, i, 1.0, 0.0, MULT, ADD)
+
+        def quads(eng, s, a, b):
+            o = tq[s][:, a:b].rearrange("p t k -> p (t k)").bitcast(F32).rearrange("p (t v) -> p t v", v=2)
+            i = pw[s][:].rearrange("p u t j -> p (u t j)").bitcast(F32).rearrange("p (u t) -> p t u", u=2)[:, a:b]
+            if eng == "v":
+                nc.vector.tensor_copy(o, i)
+            elif eng == "s":
+                nc.scalar.copy(o, i)
+            else:
+                nc.gpsimd.tensor_scalar(
+                    tq[s][:, a:b].rearrange("p t (u j) -> p t u j", u=2),
+                    pw[s][:, :, a:b].rearrange("p u t j -> p t u j"), 1.0, 0.0, MULT, ADD)
+
+        def gather(s, u, a, b):
+            nc.vector.tensor_copy(
+                sg[s][:].rearrange("p t k -> p (t k)").bitcast(U32).rearrange("p (t v) -> p t v", v=2)[:, a:b, u],
+                pw[s][:, u].rearrange("p t j -> p (t j)").bitcast(U32).indirect(offsets[:, a // 16:b // 16]),
+            )
+
+        def quant(kind, s, a, b):
+            c, sc = codes[kind, s]
+            src = sg[s] if kind == "slot" else tq[s]
+            nc.vector.quantize_mx(
+                out=c[:, a:b].bitcast(FP8X4), scales=sc[:, a:b], in_=src[:, a:b].rearrange("p t k -> p (t k)")
+            )
+
+        def first_layer(unit, s):
+            if unit < E:
+                c, sc, base, e = codes["slot", s] + (unit * 256, unit)
+            else:
+                c, sc, base, e = codes["tok", s] + ((unit - E) * 256, E)
+            for b in range(2):
+                if s == 0:
+                    acc[unit, b] = psum.tile([P, H], F32, tag="acc", bufs=6, name="acc")
+                cols = slice(base + 128 * b, base + 128 * (b + 1))
+                nc.tensor.matmul_mx(
+                    out=acc[unit, b][:],
+                    lhsT=c[:, cols].bitcast(FP8X4),
+                    lhsT_scale=sc[:, cols],
+                    rhs=w1w[s][:, e, :].bitcast(FP4X4),
+                    rhs_scale=w1s[:, e * PASSES + s, :],
+                    start=(s == 0),
+                    stop=(s == PASSES - 1),
+                )
+
+        result = keep.tile([P, T], F32, name="result")
+        st = {}
+
+        def hidden(unit, engs):
+            xt = psum.tile([P, 2, 2, 128], F32, tag="xt", bufs=1, name="xt")
+            for b in range(2):
+                ht = ring.tile([P, H], BF16, align_bytes=64, name="ht")
+                if engs[b] == "s":
+                    nc.scalar.activation(ht[:], acc[unit, b][:], RELU)
+                else:
+                    nc.vector.tensor_scalar_max(ht[:], acc[unit, b][:], 0.0)
+                words = ht[:].bitcast(F32)
+                for u in range(2):
+                    nc.tensor.transpose(xt[:, b, u, :], words[:, u:256:2], ident[:])
+            hq = ring.tile([P, 256, 4], BF16, align_bytes=64, name="hq")
+            o = hq[:].rearrange("p t k -> p (t k)").bitcast(F32).rearrange("p (b t v) -> p b t v", b=2, v=2)
+            i = xt[:].rearrange("p b u t -> p b t u")
+            if engs[2] == "s":
+                nc.scalar.copy(o, i)
+            else:
+                nc.vector.tensor_copy(o, i)
+            hc = ring.tile([P, 256], U32, align_bytes=64, name="hc")
+            hs = ring.tile([P, 256], U8, align_bytes=64, name="hs")
+            nc.vector.quantize_mx(out=hc[:].bitcast(FP8X4), scales=hs[:], in_=hq[:].rearrange("p t k -> p (t k)"))
+            e = unit if unit < E else E
+            y = psum.tile([P, 256], F32, tag="y", bufs=1, name="y")
+            nc.tensor.matmul_mx(
+                out=y[:], lhsT=w2w[:, e, :].bitcast(FP4X4), lhsT_scale=w2s[:, e, :],
+                rhs=hc[:].bitcast(FP8X4), rhs_scale=hs[:], start=True, stop=True,
+            )
+            st[unit] = y
+
+        def routed_back(unit):
+            ysb = ring.tile([P, 256], F32, name="ysb")
+            nc.scalar.copy(ysb[:], st[unit][:])
+            cols = slice(unit * C, (unit + 1) * C)
+            nc.vector.tensor_tensor(
+                scat[:].indirect(offsets[:, unit * 16:(unit + 1) * 16]), ysb[:], gate_sb[:, cols], MULT
+            )
+
+        ys = keep.tile([P, T], F32, name="ys")
+
+        def keep_y(unit):
+            nc.scalar.copy(ys[:, (unit - E) * 256:(unit - E + 1) * 256], st[unit][:])
+
+        def finish():
+            for i in range(3):
+                cols = slice(i * 256, (i + 1) * 256)
+                nc.vector.tensor_tensor(result[:, cols], ys[:, cols], scat[:, cols], ADD)
+                nc.sync.dma_start(out[:, cols], result[:, cols])
+
+        for s in range(PASSES):
+            cast("s", s, 0, 0, TA)
+            cast("g" if s else "v", s, 1, 0, TA)
+            quads("v", s, 0, TA)
+            quant("tok", s, 0, TA)
+            first_layer(2, s)
+        hidden(2, "sss")
+        keep_y(2)
+        for s in range(PASSES):
+            for u in range(2):
+                cast("s", s, u, TA, 512)
+                cast("g", s, u, 512, T)
+                gather(s, u, 0, 256)
+            quads("s", s, TA, T)
+            quant("slot", s, 0, 256)
+            first_layer(0, s)
+            quant("tok", s, TA, TA + 256)
+            quant("tok", s, TA + 256, TA + 512)
+            first_layer(3, s)
+            first_layer(4, s)
+        hidden(0, "sss")
+        for s in range(PASSES):
+            for u in range(2):
+                gather(s, u, 256, 512)
+            quant("slot", s, 256, 512)
+            first_layer(1, s)
+        hidden(3, "sss")
+        keep_y(3)
+        hidden(4, "sss")
+        keep_y(4)
+        hidden(1, "vsv")
+        routed_back(0)
+        routed_back(1)
+        finish()

@@ -59,7 +59,8 @@ def tile_moe_shr_mlp_relu_kernel(tc, xT, w1_words, w1_scales, w2_words, w2_scale
 
         w1s_i = w1s[:].rearrange("p a i -> p (a i)").bitcast(I32)
         w2s_i = w2s[:].rearrange("p a i -> p (a i)").bitcast(I32)
-        nc.vector.memset(w1s_i, 0)
+        nc.vector.memset(w1s_i[:, :576], 0)
+        nc.gpsimd.memset(w1s_i[:, 576:], 0)
         nc.gpsimd.memset(w2s_i, 0)
         w1s_i = w1s_i.rearrange("p (a i) -> p a i", i=H // 4)
         w2s_i = w2s_i.rearrange("p (a i) -> p a i", i=N // 4)
@@ -67,14 +68,14 @@ def tile_moe_shr_mlp_relu_kernel(tc, xT, w1_words, w1_scales, w2_words, w2_scale
 
         def load_scales1():
             for q in range(4):
-                nc.scalar.dma_start(
+                nc.gpsimd.dma_start(
                     w1s_i[32 * q:32 * q + 4],
                     w1_scales.bitcast(I32)[:, :, 4 * q:4 * q + 4, :].rearrange("e s q i -> q (e s) i"),
                 )
 
         def load_scales2():
             for q in range(4):
-                nc.sync.dma_start(
+                nc.scalar.dma_start(
                     w2s_i[32 * q:32 * q + 4],
                     w2_scales.bitcast(I32)[:, 0, 4 * q:4 * q + 4, :].rearrange("e q i -> q e i"),
                 )
@@ -84,23 +85,23 @@ def tile_moe_shr_mlp_relu_kernel(tc, xT, w1_words, w1_scales, w2_words, w2_scale
                 w2w[:].rearrange("p e b -> p (e b)").bitcast(I32).rearrange("p (e b) -> p e b", e=E + 1),
                 w2_words.bitcast(I32)[:, 0].rearrange("e p b -> p e b"),
             )
-
-        load_x(0, 0, 0, TA)
-        load_x(0, 1, 0, TA)
-        load_scales1()
-        load_w1(0, E, E + 1)
+        load_x(0, 0, 0, 256)
+        load_x(0, 0, 256, 512)
+        load_x(0, 0, 512, T)
+        load_x(0, 1, 0, T)
         nc.sync.dma_start(offsets[:], offs)
-        for s in (1, 2):
-            load_x(s, None, 0, TA)
-            load_w1(s, E, E + 1)
-        for s in range(PASSES):
-            load_x(s, 0, TA, T)
-            load_x(s, 1, TA, T)
-            load_w1(s, 0, E)
-            if s == 0:
-                load_w2()
-                load_scales2()
+        load_scales1()
+        load_x(1, 0, 0, T)
+        load_x(1, 1, 0, T)
+        load_x(2, 0, 0, T)
+        load_w1(0, 0, E + 1)
+        load_x(2, 1, 0, T)
+        load_w1(1, 0, E + 1)
+        load_w1(2, 0, E + 1)
+        load_w2()
         nc.sync.dma_start(gate_sb[:], gate)
+        load_scales2()
+
 
         ident = keep.tile([P, P], F32, name="ident")
         make_identity(nc, ident[:])
@@ -158,107 +159,217 @@ def tile_moe_shr_mlp_relu_kernel(tc, xT, w1_words, w1_scales, w2_words, w2_scale
                 out=c[:, a:b].bitcast(FP8X4), scales=sc[:, a:b], in_=src[:, a:b].rearrange("p t k -> p (t k)")
             )
 
-        def first_layer(unit, s):
+        def first_layer(unit, b, s):
             if unit < E:
                 c, sc, base, e = codes["slot", s] + (unit * 256, unit)
             else:
                 c, sc, base, e = codes["tok", s] + ((unit - E) * 256, E)
-            for b in range(2):
-                if s == 0:
-                    acc[unit, b] = psum.tile([P, H], F32, tag="acc", bufs=6, name="acc")
-                cols = slice(base + 128 * b, base + 128 * (b + 1))
-                nc.tensor.matmul_mx(
-                    out=acc[unit, b][:],
-                    lhsT=c[:, cols].bitcast(FP8X4),
-                    lhsT_scale=sc[:, cols],
-                    rhs=w1w[s][:, e, :].bitcast(FP4X4),
-                    rhs_scale=w1s[:, e * PASSES + s, :],
-                    start=(s == 0),
-                    stop=(s == PASSES - 1),
-                )
+            if s == 0:
+                acc[unit, b] = psum.tile([P, H], F32, tag="acc", bufs=6, name="acc")
+            cols = slice(base + 128 * b, base + 128 * (b + 1))
+            nc.tensor.matmul_mx(
+                out=acc[unit, b][:],
+                lhsT=c[:, cols].bitcast(FP8X4),
+                lhsT_scale=sc[:, cols],
+                rhs=w1w[s][:, e, :].bitcast(FP4X4),
+                rhs_scale=w1s[:, e * PASSES + s, :],
+                start=(s == 0),
+                stop=(s == PASSES - 1),
+            )
 
+        ht = {}
+        hq = {}
+        hc = {}
+        hs = {}
+        xt = {}
+        y = {}
+        ysb = {}
+        for unit in range(5):
+            for b in range(2):
+                ht[unit, b] = keep.tile([P, H], BF16, align_bytes=64, name=f"ht{unit}{b}")
+            hq[unit] = keep.tile([P, 256, 4], BF16, align_bytes=64, name=f"hq{unit}")
+            hc[unit] = keep.tile([P, 256], U32, align_bytes=64, name=f"hc{unit}")
+            hs[unit] = keep.tile([P, 256], U8, align_bytes=64, name=f"hs{unit}")
+            ysb[unit] = keep.tile([P, 256], F32, name=f"ysb{unit}")
         result = keep.tile([P, T], F32, name="result")
-        st = {}
 
-        def hidden(unit, engs):
-            xt = psum.tile([P, 2, 2, 128], F32, tag="xt", bufs=1, name="xt")
-            for b in range(2):
-                ht = ring.tile([P, H], BF16, align_bytes=64, name="ht")
-                if engs[b] == "s":
-                    nc.scalar.activation(ht[:], acc[unit, b][:], RELU)
-                else:
-                    nc.vector.tensor_scalar_max(ht[:], acc[unit, b][:], 0.0)
-                words = ht[:].bitcast(F32)
-                for u in range(2):
-                    nc.tensor.transpose(xt[:, b, u, :], words[:, u:256:2], ident[:])
-            hq = ring.tile([P, 256, 4], BF16, align_bytes=64, name="hq")
-            o = hq[:].rearrange("p t k -> p (t k)").bitcast(F32).rearrange("p (b t v) -> p b t v", b=2, v=2)
-            i = xt[:].rearrange("p b u t -> p b t u")
-            if engs[2] == "s":
+        def relu(eng, unit, b):
+            if eng == "s":
+                nc.scalar.activation(ht[unit, b][:], acc[unit, b][:], RELU)
+            else:
+                nc.vector.tensor_scalar_max(ht[unit, b][:], acc[unit, b][:], 0.0)
+
+        def turn(unit, b):
+            if unit not in xt:
+                xt[unit] = psum.tile([P, 2, 2, 128], F32, tag="xt", bufs=1, name="xt")
+            words = ht[unit, b][:].bitcast(F32)
+            for u in range(2):
+                nc.tensor.transpose(xt[unit][:, b, u, :], words[:, u:256:2], ident[:])
+
+        def spread(eng, unit):
+            o = hq[unit][:].rearrange("p t k -> p (t k)").bitcast(F32).rearrange("p (b t v) -> p b t v", b=2, v=2)
+            i = xt[unit][:].rearrange("p b u t -> p b t u")
+            if eng == "s":
                 nc.scalar.copy(o, i)
             else:
                 nc.vector.tensor_copy(o, i)
-            hc = ring.tile([P, 256], U32, align_bytes=64, name="hc")
-            hs = ring.tile([P, 256], U8, align_bytes=64, name="hs")
-            nc.vector.quantize_mx(out=hc[:].bitcast(FP8X4), scales=hs[:], in_=hq[:].rearrange("p t k -> p (t k)"))
-            e = unit if unit < E else E
-            y = psum.tile([P, 256], F32, tag="y", bufs=1, name="y")
-            nc.tensor.matmul_mx(
-                out=y[:], lhsT=w2w[:, e, :].bitcast(FP4X4), lhsT_scale=w2s[:, e, :],
-                rhs=hc[:].bitcast(FP8X4), rhs_scale=hs[:], start=True, stop=True,
-            )
-            st[unit] = y
 
-        def routed_back(unit):
-            ysb = ring.tile([P, 256], F32, name="ysb")
-            nc.scalar.copy(ysb[:], st[unit][:])
+        def quant_h(unit):
+            nc.vector.quantize_mx(
+                out=hc[unit][:].bitcast(FP8X4), scales=hs[unit][:], in_=hq[unit][:].rearrange("p t k -> p (t k)")
+            )
+
+        def second_layer(unit):
+            e = min(unit, E)
+            y[unit] = psum.tile([P, 256], F32, tag="y", bufs=1, name="y")
+            nc.tensor.matmul_mx(
+                out=y[unit][:], lhsT=w2w[:, e, :].bitcast(FP4X4), lhsT_scale=w2s[:, e, :],
+                rhs=hc[unit][:].bitcast(FP8X4), rhs_scale=hs[unit][:], start=True, stop=True,
+            )
+
+        def take_y(eng, unit):
+            if eng == "s":
+                nc.scalar.copy(ysb[unit][:], y[unit][:])
+            else:
+                nc.vector.tensor_copy(ysb[unit][:], y[unit][:])
+
+        def scatter(unit):
             cols = slice(unit * C, (unit + 1) * C)
             nc.vector.tensor_tensor(
-                scat[:].indirect(offsets[:, unit * 16:(unit + 1) * 16]), ysb[:], gate_sb[:, cols], MULT
+                scat[:].indirect(offsets[:, unit * 16:(unit + 1) * 16]), ysb[unit][:], gate_sb[:, cols], MULT
             )
 
-        ys = keep.tile([P, T], F32, name="ys")
+        def finish(j):
+            cols = slice(j * 256, (j + 1) * 256)
+            nc.vector.tensor_tensor(result[:, cols], ysb[E + j][:], scat[:, cols], ADD)
+            nc.sync.dma_start(out[:, cols], result[:, cols])
 
-        def keep_y(unit):
-            nc.scalar.copy(ys[:, (unit - E) * 256:(unit - E + 1) * 256], st[unit][:])
-
-        def finish():
-            for i in range(3):
-                cols = slice(i * 256, (i + 1) * 256)
-                nc.vector.tensor_tensor(result[:, cols], ys[:, cols], scat[:, cols], ADD)
-                nc.sync.dma_start(out[:, cols], result[:, cols])
-
-        for s in range(PASSES):
-            cast("s", s, 0, 0, TA)
-            cast("g" if s else "v", s, 1, 0, TA)
-            quads("v", s, 0, TA)
-            quant("tok", s, 0, TA)
-            first_layer(2, s)
-        hidden(2, "sss")
-        keep_y(2)
-        for s in range(PASSES):
-            for u in range(2):
-                cast("s", s, u, TA, 512)
-                cast("g", s, u, 512, T)
-                gather(s, u, 0, 256)
-            quads("s", s, TA, T)
-            quant("slot", s, 0, 256)
-            first_layer(0, s)
-            quant("tok", s, TA, TA + 256)
-            quant("tok", s, TA + 256, TA + 512)
-            first_layer(3, s)
-            first_layer(4, s)
-        hidden(0, "sss")
-        for s in range(PASSES):
-            for u in range(2):
-                gather(s, u, 256, 512)
-            quant("slot", s, 256, 512)
-            first_layer(1, s)
-        hidden(3, "sss")
-        keep_y(3)
-        hidden(4, "sss")
-        keep_y(4)
-        hidden(1, "vsv")
-        routed_back(0)
-        routed_back(1)
-        finish()
+        cast("s", 0, 0, 0, 256)
+        cast("v", 0, 0, 256, 512)
+        cast("s", 0, 0, 512, 768)
+        cast("v", 0, 1, 256, 512)
+        cast("s", 0, 1, 0, 256)
+        gather(0, 0, 256, 512)
+        quads("s", 0, 256, 512)
+        cast("v", 0, 1, 512, 768)
+        quads("v", 0, 0, 256)
+        gather(0, 0, 0, 256)
+        quads("s", 0, 512, 768)
+        cast("s", 1, 0, 256, 512)
+        gather(0, 1, 0, 256)
+        cast("s", 1, 0, 0, 256)
+        quant("tok", 0, 512, 768)
+        quant("tok", 0, 0, 256)
+        cast("s", 1, 0, 512, 768)
+        quant("slot", 0, 0, 256)
+        gather(0, 1, 256, 512)
+        cast("s", 1, 1, 0, 256)
+        gather(1, 0, 0, 256)
+        cast("s", 1, 1, 256, 512)
+        quant("slot", 0, 256, 512)
+        cast("s", 1, 1, 512, 768)
+        gather(1, 0, 256, 512)
+        quads("s", 1, 256, 512)
+        first_layer(0, 0, 0)
+        quant("tok", 0, 256, 512)
+        quads("s", 1, 512, 768)
+        first_layer(0, 1, 0)
+        gather(1, 1, 256, 512)
+        first_layer(4, 1, 0)
+        cast("s", 2, 0, 512, 768)
+        quant("tok", 1, 256, 512)
+        first_layer(1, 0, 0)
+        quant("tok", 1, 512, 768)
+        first_layer(1, 1, 0)
+        quads("s", 1, 0, 256)
+        quant("slot", 1, 256, 512)
+        first_layer(4, 0, 0)
+        cast("v", 2, 1, 512, 768)
+        cast("s", 2, 1, 0, 256)
+        gather(1, 1, 0, 256)
+        first_layer(4, 0, 1)
+        cast("s", 2, 1, 256, 512)
+        first_layer(1, 0, 1)
+        quads("v", 2, 512, 768)
+        quant("tok", 1, 0, 256)
+        first_layer(1, 1, 1)
+        cast("s", 2, 0, 256, 512)
+        quant("slot", 1, 0, 256)
+        first_layer(4, 1, 1)
+        cast("s", 2, 0, 0, 256)
+        quant("tok", 2, 512, 768)
+        gather(2, 1, 0, 256)
+        first_layer(0, 0, 1)
+        quads("s", 2, 256, 512)
+        first_layer(4, 0, 2)
+        gather(2, 0, 0, 256)
+        first_layer(4, 1, 2)
+        first_layer(0, 1, 1)
+        relu("s", 4, 0)
+        quant("tok", 2, 256, 512)
+        gather(2, 0, 256, 512)
+        relu("s", 4, 1)
+        turn(4, 0)
+        quant("slot", 2, 0, 256)
+        first_layer(2, 1, 0)
+        quads("v", 2, 0, 256)
+        turn(4, 1)
+        gather(2, 1, 256, 512)
+        first_layer(0, 0, 2)
+        first_layer(0, 1, 2)
+        spread("s", 4)
+        quant("tok", 2, 0, 256)
+        first_layer(2, 1, 1)
+        relu("v", 0, 0)
+        first_layer(3, 0, 0)
+        relu("s", 0, 1)
+        first_layer(2, 1, 2)
+        quant("slot", 2, 256, 512)
+        first_layer(3, 0, 1)
+        quant_h(4)
+        turn(0, 0)
+        relu("v", 2, 1)
+        first_layer(1, 0, 2)
+        turn(0, 1)
+        first_layer(1, 1, 2)
+        relu("s", 1, 0)
+        first_layer(3, 1, 0)
+        spread("v", 0)
+        first_layer(3, 0, 2)
+        relu("s", 1, 1)
+        first_layer(3, 1, 1)
+        quant_h(0)
+        turn(1, 0)
+        relu("v", 3, 0)
+        second_layer(4)
+        turn(1, 1)
+        first_layer(3, 1, 2)
+        take_y("s", 4)
+        first_layer(2, 0, 0)
+        spread("s", 1)
+        second_layer(0)
+        first_layer(2, 0, 1)
+        relu("s", 3, 1)
+        take_y("v", 0)
+        first_layer(2, 0, 2)
+        quant_h(1)
+        turn(3, 0)
+        scatter(0)
+        relu("s", 2, 0)
+        turn(3, 1)
+        second_layer(1)
+        spread("s", 3)
+        take_y("s", 1)
+        quant_h(3)
+        turn(2, 0)
+        scatter(1)
+        turn(2, 1)
+        second_layer(3)
+        spread("s", 2)
+        take_y("s", 3)
+        quant_h(2)
+        finish(2)
+        finish(1)
+        second_layer(2)
+        take_y("s", 2)
+        finish(0)

@@ -4,10 +4,15 @@ import concourse.mybir as mybir
 from concourse.masks import make_identity
 
 K, T, E, C, H, N = 1536, 768, 2, 256, 512, 128
+
 P = 128
 S = E * C
-PASSES = K // 512
-TA = 256
+K_PASS = 512
+PASSES = K // K_PASS
+QUADRANTS = 4
+SHARED = E
+UNIT = 2 * P
+
 FLOPS = 2 * (S + T) * (K * H + H * N)
 
 F32 = mybir.dt.float32
@@ -18,358 +23,307 @@ U16 = mybir.dt.uint16
 U8 = mybir.dt.uint8
 FP8X4 = mybir.dt.float8_e4m3fn_x4
 FP4X4 = mybir.dt.float4_e2m1fn_x4
+
 RELU = mybir.ActivationFunctionType.Relu
-COPY = mybir.ActivationFunctionType.Copy
 MULT = mybir.AluOpType.mult
 ADD = mybir.AluOpType.add
 
+SPLIT = 512
 
-def tile_moe_shr_mlp_relu_kernel(tc, xT, w1_words, w1_scales, w2_words, w2_scales, gate, offs, out):
+STREAMED = (("token", 4), ("token", 5), ("slot", 0), ("slot", 1), ("slot", 3))
+
+
+def tile_moe_shr_mlp_relu_kernel(
+    tc, xT, w1_words, w1_scales, w2_words, w2_scales, gate, offs, out
+):
     nc = tc.nc
     with ExitStack() as ctx:
         keep = ctx.enter_context(tc.tile_pool(name="keep", bufs=1))
-        ring = ctx.enter_context(tc.tile_pool(name="ring", bufs=4))
         psum = ctx.enter_context(tc.psum_pool(name="psum", bufs=1))
 
-        xraw = {}
-        w1w = {}
         offsets = keep.tile([P, S // 16], U16, name="offsets")
-        w1s = keep.tile([P, (E + 1) * PASSES, H], U8, align_bytes=64, name="w1s")
-        w2s = keep.tile([P, E + 1, N], U8, align_bytes=64, name="w2s")
-        w2w = keep.tile([P, E + 1, 2 * N], U8, align_bytes=64, name="w2w")
         gate_sb = keep.tile([P, S], F32, name="gate_sb")
+        w2_codes = keep.tile([P, E + 1, 2 * N], U8, align_bytes=64, name="w2_codes")
+        w1_planes = keep.tile([P, (E + 1) * PASSES, H], U8, align_bytes=64, name="w1_planes")
+        w2_planes = keep.tile([P, E + 1, N], U8, align_bytes=64, name="w2_planes")
+        ident = keep.tile([P, P], F32, name="ident")
+        routed = keep.tile([P, T], F32, name="routed")
+        routed_y = keep.tile([P, S], F32, name="routed_y")
+        result = keep.tile([P, T], F32, name="result")
+
+        x_raw, w1_codes, x_pairs, slot_pairs = {}, {}, {}, {}
+        quads, codes, planes = {}, {}, {}
         for s in range(PASSES):
-            xraw[s] = keep.tile([P, 4, T], F32, name=f"xraw{s}")
-            w1w[s] = keep.tile([P, E + 1, 2 * H], U8, align_bytes=64, name=f"w1w{s}")
-
-        def load_x(s, u, a, b):
-            src = xT[512 * s:512 * (s + 1), :].rearrange("(p j) t -> p j t", j=4)
-            rows = slice(0, 4) if u is None else slice(2 * u, 2 * u + 2)
-            nc.sync.dma_start(xraw[s][:, rows, a:b], src[:, rows, a:b])
-
-        def load_w1(s, e0, e1):
-            nc.sync.dma_start(
-                w1w[s][:, e0:e1].rearrange("p e b -> p (e b)").bitcast(I32).rearrange("p (e b) -> p e b", e=e1 - e0),
-                w1_words.bitcast(I32)[e0:e1, s].rearrange("e p b -> p e b"),
-            )
+            x_raw[s] = keep.tile([P, 4, T], F32, name=f"x_raw{s}")
+            w1_codes[s] = keep.tile([P, E + 1, 2 * H], U8, align_bytes=64, name=f"w1_codes{s}")
+            x_pairs[s] = keep.tile([P, 2, T, 2], BF16, align_bytes=64, name=f"x_pairs{s}")
+            slot_pairs[s] = keep.tile([P, 2, S, 2], BF16, align_bytes=64, name=f"slot_pairs{s}")
+        h_rows, h_quads, h_codes, h_planes = {}, {}, {}, {}
+        for kind, n in (("slot", S), ("token", T)):
+            for s in range(PASSES):
+                quads[kind, s] = keep.tile([P, n, 4], BF16, align_bytes=64, name=f"{kind}_quads{s}")
+                codes[kind, s] = keep.tile([P, n], U32, align_bytes=64, name=f"{kind}_codes{s}")
+                planes[kind, s] = keep.tile([P, n], U8, align_bytes=64, name=f"{kind}_planes{s}")
+            h_rows[kind] = keep.tile([P, n // P, H], BF16, align_bytes=64, name=f"{kind}_h_rows")
+            h_quads[kind] = keep.tile([P, n, 4], BF16, align_bytes=64, name=f"{kind}_h_quads")
+            h_codes[kind] = keep.tile([P, n], U32, align_bytes=64, name=f"{kind}_h_codes")
+            h_planes[kind] = keep.tile([P, n], U8, align_bytes=64, name=f"{kind}_h_planes")
 
         warm = keep.tile([P, 1], F32, name="warm")
         nc.vector.memset(warm[:], 0.0)
         nc.scalar.activation(warm[:], warm[:], RELU)
 
-        w1s_i = w1s[:].rearrange("p a i -> p (a i)").bitcast(I32)
-        w2s_i = w2s[:].rearrange("p a i -> p (a i)").bitcast(I32)
-        nc.vector.memset(w1s_i[:, :576], 0)
-        nc.gpsimd.memset(w1s_i[:, 576:], 0)
-        nc.gpsimd.memset(w2s_i, 0)
-        w1s_i = w1s_i.rearrange("p (a i) -> p a i", i=H // 4)
-        w2s_i = w2s_i.rearrange("p (a i) -> p a i", i=N // 4)
+        w1_plane_words = w1_planes[:].rearrange("p a i -> p (a i)").bitcast(I32)
+        w2_plane_words = w2_planes[:].rearrange("p a i -> p (a i)").bitcast(I32)
+        half = (E + 1) * PASSES * H // 4 // 2
+        nc.vector.memset(w1_plane_words[:, :half], 0)
+        nc.gpsimd.memset(w1_plane_words[:, half:], 0)
+        nc.gpsimd.memset(w2_plane_words, 0)
 
+        def load_x(s, u, first, end):
+            rows = xT[K_PASS * s : K_PASS * (s + 1), :].rearrange("(p d) t -> p d t", d=4)
+            pair = slice(2 * u, 2 * u + 2)
+            nc.sync.dma_start(x_raw[s][:, pair, first:end], rows[:, pair, first:end])
 
-        def load_scales1():
-            for q in range(4):
-                nc.gpsimd.dma_start(
-                    w1s_i[32 * q:32 * q + 4],
-                    w1_scales.bitcast(I32)[:, :, 4 * q:4 * q + 4, :].rearrange("e s q i -> q (e s) i"),
-                )
-
-        def load_scales2():
-            for q in range(4):
-                nc.scalar.dma_start(
-                    w2s_i[32 * q:32 * q + 4],
-                    w2_scales.bitcast(I32)[:, 0, 4 * q:4 * q + 4, :].rearrange("e q i -> q e i"),
-                )
-
-        def load_w2():
+        def load_codes(tile, words):
+            experts = E + 1
             nc.sync.dma_start(
-                w2w[:].rearrange("p e b -> p (e b)").bitcast(I32).rearrange("p (e b) -> p e b", e=E + 1),
-                w2_words.bitcast(I32)[:, 0].rearrange("e p b -> p e b"),
+                tile[:].rearrange("p e b -> p (e b)").bitcast(I32).rearrange("p (e b) -> p e b", e=experts),
+                words.rearrange("e p b -> p e b"),
             )
-        load_x(0, 0, 0, 256)
-        load_x(0, 0, 256, 512)
-        load_x(0, 0, 512, T)
-        load_x(0, 1, 0, T)
+
+        for first in range(0, T, UNIT):
+            load_x(0, 0, first, first + UNIT)
         nc.sync.dma_start(offsets[:], offs)
-        load_scales1()
+        for q in range(QUADRANTS):
+            nc.gpsimd.dma_start(
+                w1_plane_words.rearrange("p (a i) -> p a i", i=H // 4)[32 * q : 32 * q + 4],
+                w1_scales.bitcast(I32)[:, :, 4 * q : 4 * q + 4, :].rearrange("e s q i -> q (e s) i"),
+            )
+        load_x(0, 1, 0, T)
         load_x(1, 0, 0, T)
         load_x(1, 1, 0, T)
         load_x(2, 0, 0, T)
-        load_w1(0, 0, E + 1)
+        load_codes(w1_codes[0], w1_words.bitcast(I32)[:, 0])
         load_x(2, 1, 0, T)
-        load_w1(1, 0, E + 1)
-        load_w1(2, 0, E + 1)
-        load_w2()
+        load_codes(w1_codes[1], w1_words.bitcast(I32)[:, 1])
+        load_codes(w1_codes[2], w1_words.bitcast(I32)[:, 2])
+        load_codes(w2_codes, w2_words.bitcast(I32)[:, 0])
         nc.sync.dma_start(gate_sb[:], gate)
-        load_scales2()
+        for q in range(QUADRANTS):
+            nc.sync.dma_start(
+                w2_plane_words.rearrange("p (a i) -> p a i", i=N // 4)[32 * q : 32 * q + 4],
+                w2_scales.bitcast(I32)[:, 0, 4 * q : 4 * q + 4, :].rearrange("e q i -> q e i"),
+            )
 
-
-        ident = keep.tile([P, P], F32, name="ident")
         make_identity(nc, ident[:])
-        scat = keep.tile([P, T], F32, name="scat")
-        nc.gpsimd.memset(scat[:], 0.0)
+        nc.gpsimd.memset(routed[:], 0.0)
 
-        acc = {}
-        codes = {}
-        pw = {}
-        sg = {}
-        tq = {}
-        for s in range(PASSES):
-            pw[s] = keep.tile([P, 2, T, 2], BF16, align_bytes=64, name=f"pw{s}")
-            sg[s] = keep.tile([P, S, 4], BF16, align_bytes=64, name=f"sg{s}")
-            tq[s] = keep.tile([P, T, 4], BF16, align_bytes=64, name=f"tq{s}")
-            c = keep.tile([P, T], U32, align_bytes=64, name=f"tc{s}")
-            sc = keep.tile([P, T], U8, align_bytes=64, name=f"ts{s}")
-            codes["tok", s] = (c, sc)
-            c = keep.tile([P, S], U32, align_bytes=64, name=f"sc{s}")
-            sc = keep.tile([P, S], U8, align_bytes=64, name=f"ss{s}")
-            codes["slot", s] = (c, sc)
-
-        def cast(eng, s, u, a, b):
-            o = pw[s][:, u, a:b, :]
-            i = xraw[s][:, 2 * u:2 * u + 2, a:b].rearrange("p j t -> p t j")
-            if eng == "v":
-                nc.vector.tensor_copy(o, i)
-            elif eng == "s":
-                nc.scalar.copy(o, i)
+        def copy(engine, dst, src):
+            if engine == "vector":
+                nc.vector.tensor_copy(dst, src)
             else:
-                nc.gpsimd.tensor_scalar(o, i, 1.0, 0.0, MULT, ADD)
+                nc.scalar.copy(dst, src)
 
-        def quads(eng, s, a, b):
-            o = tq[s][:, a:b].rearrange("p t k -> p (t k)").bitcast(F32).rearrange("p (t v) -> p t v", v=2)
-            i = pw[s][:].rearrange("p u t j -> p (u t j)").bitcast(F32).rearrange("p (u t) -> p t u", u=2)[:, a:b]
-            if eng == "v":
-                nc.vector.tensor_copy(o, i)
-            elif eng == "s":
-                nc.scalar.copy(o, i)
-            else:
-                nc.gpsimd.tensor_scalar(
-                    tq[s][:, a:b].rearrange("p t (u j) -> p t u j", u=2),
-                    pw[s][:, :, a:b].rearrange("p u t j -> p t u j"), 1.0, 0.0, MULT, ADD)
+        def as_words(tile, columns):
+            return tile[:, columns].rearrange("p c d -> p (c d)").bitcast(F32).rearrange("p (c u) -> p c u", u=2)
 
-        def gather(s, u, a, b):
+        def round_x(engine, s, u, first, end):
+            copy(
+                engine,
+                x_pairs[s][:, u, first:end, :],
+                x_raw[s][:, 2 * u : 2 * u + 2, first:end].rearrange("p d t -> p t d"),
+            )
+
+        def gather(s, u, first, end):
             nc.vector.tensor_copy(
-                sg[s][:].rearrange("p t k -> p (t k)").bitcast(U32).rearrange("p (t v) -> p t v", v=2)[:, a:b, u],
-                pw[s][:, u].rearrange("p t j -> p (t j)").bitcast(U32).indirect(offsets[:, a // 16:b // 16]),
+                slot_pairs[s][:, u, first:end].rearrange("p c d -> p (c d)").bitcast(U32),
+                x_pairs[s][:, u].rearrange("p t d -> p (t d)").bitcast(U32).indirect(offsets[:, first // 16 : end // 16]),
             )
 
-        def quant(kind, s, a, b):
-            c, sc = codes[kind, s]
-            src = sg[s] if kind == "slot" else tq[s]
+        def interleave(engine, kind, s, first, end):
+            pairs = slot_pairs[s] if kind == "slot" else x_pairs[s]
+            words = pairs[:].rearrange("p u c d -> p (u c d)").bitcast(F32).rearrange("p (u c) -> p c u", u=2)
+            copy(engine, as_words(quads[kind, s], slice(first, end)), words[:, first:end])
+
+        def quantise_x(kind, s, first, end):
             nc.vector.quantize_mx(
-                out=c[:, a:b].bitcast(FP8X4), scales=sc[:, a:b], in_=src[:, a:b].rearrange("p t k -> p (t k)")
+                out=codes[kind, s][:, first:end].bitcast(FP8X4),
+                scales=planes[kind, s][:, first:end],
+                in_=quads[kind, s][:, first:end].rearrange("p c d -> p (c d)"),
             )
 
-        def first_layer(unit, b, s):
-            if unit < E:
-                c, sc, base, e = codes["slot", s] + (unit * 256, unit)
-            else:
-                c, sc, base, e = codes["tok", s] + ((unit - E) * 256, E)
+        def expert_of(kind, block):
+            return block * P // C if kind == "slot" else SHARED
+
+        bank = {}
+
+        def first_layer(kind, block, s):
             if s == 0:
-                acc[unit, b] = psum.tile([P, H], F32, tag="acc", bufs=6, name="acc")
-            cols = slice(base + 128 * b, base + 128 * (b + 1))
+                bank[kind, block] = psum.tile([P, H], F32, tag="sums", bufs=5, name="sums")
+            e = expert_of(kind, block)
+            columns = slice(P * block, P * (block + 1))
             nc.tensor.matmul_mx(
-                out=acc[unit, b][:],
-                lhsT=c[:, cols].bitcast(FP8X4),
-                lhsT_scale=sc[:, cols],
-                rhs=w1w[s][:, e, :].bitcast(FP4X4),
-                rhs_scale=w1s[:, e * PASSES + s, :],
+                out=bank[kind, block][:],
+                lhsT=codes[kind, s][:, columns].bitcast(FP8X4),
+                lhsT_scale=planes[kind, s][:, columns],
+                rhs=w1_codes[s][:, e, :].bitcast(FP4X4),
+                rhs_scale=w1_planes[:, e * PASSES + s, :],
                 start=(s == 0),
                 stop=(s == PASSES - 1),
             )
 
-        ht = {}
-        hq = {}
-        hc = {}
-        hs = {}
-        xt = {}
-        y = {}
-        ysb = {}
-        for unit in range(5):
-            for b in range(2):
-                ht[unit, b] = keep.tile([P, H], BF16, align_bytes=64, name=f"ht{unit}{b}")
-            hq[unit] = keep.tile([P, 256, 4], BF16, align_bytes=64, name=f"hq{unit}")
-            hc[unit] = keep.tile([P, 256], U32, align_bytes=64, name=f"hc{unit}")
-            hs[unit] = keep.tile([P, 256], U8, align_bytes=64, name=f"hs{unit}")
-            ysb[unit] = keep.tile([P, 256], F32, name=f"ysb{unit}")
-        result = keep.tile([P, T], F32, name="result")
-
-        def relu(eng, unit, b):
-            if eng == "s":
-                nc.scalar.activation(ht[unit, b][:], acc[unit, b][:], RELU)
+        def relu(engine, kind, block):
+            if engine == "vector":
+                nc.vector.tensor_scalar_max(h_rows[kind][:, block], bank[kind, block][:], 0.0)
             else:
-                nc.vector.tensor_scalar_max(ht[unit, b][:], acc[unit, b][:], 0.0)
+                nc.scalar.activation(h_rows[kind][:, block], bank[kind, block][:], RELU)
 
-        def turn(unit, b):
-            if unit not in xt:
-                xt[unit] = psum.tile([P, 2, 2, 128], F32, tag="xt", bufs=1, name="xt")
-            words = ht[unit, b][:].bitcast(F32)
+        turned = {}
+
+        def turn(kind, block):
+            unit, b = divmod(block, 2)
+            if b == 0:
+                turned[kind, unit] = psum.tile([P, 2, 2, P], F32, tag="turned", bufs=2, name="turned")
+            words = h_rows[kind][:, block].bitcast(F32)
             for u in range(2):
-                nc.tensor.transpose(xt[unit][:, b, u, :], words[:, u:256:2], ident[:])
+                nc.tensor.transpose(turned[kind, unit][:, b, u, :], words[:, u : H // 2 : 2], ident[:])
 
-        def spread(eng, unit):
-            o = hq[unit][:].rearrange("p t k -> p (t k)").bitcast(F32).rearrange("p (b t v) -> p b t v", b=2, v=2)
-            i = xt[unit][:].rearrange("p b u t -> p b t u")
-            if eng == "s":
-                nc.scalar.copy(o, i)
-            else:
-                nc.vector.tensor_copy(o, i)
+        def unit_columns(unit):
+            return slice(UNIT * unit, UNIT * (unit + 1))
 
-        def quant_h(unit):
+        def spread(kind, unit):
+            nc.scalar.copy(
+                as_words(h_quads[kind], unit_columns(unit)).rearrange("p (b c) u -> p b c u", b=2),
+                turned[kind, unit][:].rearrange("p b u c -> p b c u"),
+            )
+
+        def quantise_h(kind, unit):
+            columns = unit_columns(unit)
             nc.vector.quantize_mx(
-                out=hc[unit][:].bitcast(FP8X4), scales=hs[unit][:], in_=hq[unit][:].rearrange("p t k -> p (t k)")
+                out=h_codes[kind][:, columns].bitcast(FP8X4),
+                scales=h_planes[kind][:, columns],
+                in_=h_quads[kind][:, columns].rearrange("p c d -> p (c d)"),
             )
 
-        def second_layer(unit):
-            e = min(unit, E)
-            y[unit] = psum.tile([P, 256], F32, tag="y", bufs=1, name="y")
-            nc.tensor.matmul_mx(
-                out=y[unit][:], lhsT=w2w[:, e, :].bitcast(FP4X4), lhsT_scale=w2s[:, e, :],
-                rhs=hc[unit][:].bitcast(FP8X4), rhs_scale=hs[unit][:], start=True, stop=True,
-            )
+        y = {}
 
-        def take_y(eng, unit):
-            if eng == "s":
-                nc.scalar.copy(ysb[unit][:], y[unit][:])
+        def second_layer(kind, unit):
+            columns = unit_columns(unit)
+            e = expert_of(kind, 2 * unit)
+            if kind == "slot":
+                y[kind, unit] = psum.tile([P, UNIT], F32, tag="y", bufs=1, name="y")
             else:
-                nc.vector.tensor_copy(ysb[unit][:], y[unit][:])
+                y[kind, unit] = psum.tile([P, UNIT], F32, tag="sums", bufs=5, name="ys")
+            nc.tensor.matmul_mx(
+                out=y[kind, unit][:],
+                lhsT=w2_codes[:, e, :].bitcast(FP4X4),
+                lhsT_scale=w2_planes[:, e, :],
+                rhs=h_codes[kind][:, columns].bitcast(FP8X4),
+                rhs_scale=h_planes[kind][:, columns],
+                start=True,
+                stop=True,
+            )
+
+        def take_y(unit):
+            nc.scalar.copy(routed_y[:, unit_columns(unit)], y["slot", unit][:])
 
         def scatter(unit):
-            cols = slice(unit * C, (unit + 1) * C)
+            columns = unit_columns(unit)
             nc.vector.tensor_tensor(
-                scat[:].indirect(offsets[:, unit * 16:(unit + 1) * 16]), ysb[unit][:], gate_sb[:, cols], MULT
+                routed[:].indirect(offsets[:, UNIT // 16 * unit : UNIT // 16 * (unit + 1)]),
+                routed_y[:, columns],
+                gate_sb[:, columns],
+                MULT,
             )
 
-        def finish(j):
-            cols = slice(j * 256, (j + 1) * 256)
-            nc.vector.tensor_tensor(result[:, cols], ysb[E + j][:], scat[:, cols], ADD)
-            nc.sync.dma_start(out[:, cols], result[:, cols])
+        def finish(unit):
+            columns = unit_columns(unit)
+            nc.vector.tensor_tensor(result[:, columns], y["token", unit][:], routed[:, columns], ADD)
+            nc.sync.dma_start(out[:, columns], result[:, columns])
 
-        cast("s", 0, 0, 0, 256)
-        cast("v", 0, 0, 256, 512)
-        cast("s", 0, 0, 512, 768)
-        cast("v", 0, 1, 256, 512)
-        cast("s", 0, 1, 0, 256)
-        gather(0, 0, 256, 512)
-        quads("s", 0, 256, 512)
-        cast("v", 0, 1, 512, 768)
-        quads("v", 0, 0, 256)
-        gather(0, 0, 0, 256)
-        quads("s", 0, 512, 768)
-        cast("s", 1, 0, 256, 512)
-        gather(0, 1, 0, 256)
-        cast("s", 1, 0, 0, 256)
-        quant("tok", 0, 512, 768)
-        quant("tok", 0, 0, 256)
-        cast("s", 1, 0, 512, 768)
-        quant("slot", 0, 0, 256)
-        gather(0, 1, 256, 512)
-        cast("s", 1, 1, 0, 256)
-        gather(1, 0, 0, 256)
-        cast("s", 1, 1, 256, 512)
-        quant("slot", 0, 256, 512)
-        cast("s", 1, 1, 512, 768)
-        gather(1, 0, 256, 512)
-        quads("s", 1, 256, 512)
-        first_layer(0, 0, 0)
-        quant("tok", 0, 256, 512)
-        quads("s", 1, 512, 768)
-        first_layer(0, 1, 0)
-        gather(1, 1, 256, 512)
-        first_layer(4, 1, 0)
-        cast("s", 2, 0, 512, 768)
-        quant("tok", 1, 256, 512)
-        first_layer(1, 0, 0)
-        quant("tok", 1, 512, 768)
-        first_layer(1, 1, 0)
-        quads("s", 1, 0, 256)
-        quant("slot", 1, 256, 512)
-        first_layer(4, 0, 0)
-        cast("v", 2, 1, 512, 768)
-        cast("s", 2, 1, 0, 256)
-        gather(1, 1, 0, 256)
-        first_layer(4, 0, 1)
-        cast("s", 2, 1, 256, 512)
-        first_layer(1, 0, 1)
-        quads("v", 2, 512, 768)
-        quant("tok", 1, 0, 256)
-        first_layer(1, 1, 1)
-        cast("s", 2, 0, 256, 512)
-        quant("slot", 1, 0, 256)
-        first_layer(4, 1, 1)
-        cast("s", 2, 0, 0, 256)
-        quant("tok", 2, 512, 768)
-        gather(2, 1, 0, 256)
-        first_layer(0, 0, 1)
-        quads("s", 2, 256, 512)
-        first_layer(4, 0, 2)
-        gather(2, 0, 0, 256)
-        first_layer(4, 1, 2)
-        first_layer(0, 1, 1)
-        relu("s", 4, 0)
-        quant("tok", 2, 256, 512)
-        gather(2, 0, 256, 512)
-        relu("s", 4, 1)
-        turn(4, 0)
-        quant("slot", 2, 0, 256)
-        first_layer(2, 1, 0)
-        quads("v", 2, 0, 256)
-        turn(4, 1)
-        gather(2, 1, 256, 512)
-        first_layer(0, 0, 2)
-        first_layer(0, 1, 2)
-        spread("s", 4)
-        quant("tok", 2, 0, 256)
-        first_layer(2, 1, 1)
-        relu("v", 0, 0)
-        first_layer(3, 0, 0)
-        relu("s", 0, 1)
-        first_layer(2, 1, 2)
-        quant("slot", 2, 256, 512)
-        first_layer(3, 0, 1)
-        quant_h(4)
-        turn(0, 0)
-        relu("v", 2, 1)
-        first_layer(1, 0, 2)
-        turn(0, 1)
-        first_layer(1, 1, 2)
-        relu("s", 1, 0)
-        first_layer(3, 1, 0)
-        spread("v", 0)
-        first_layer(3, 0, 2)
-        relu("s", 1, 1)
-        first_layer(3, 1, 1)
-        quant_h(0)
-        turn(1, 0)
-        relu("v", 3, 0)
-        second_layer(4)
-        turn(1, 1)
-        first_layer(3, 1, 2)
-        take_y("s", 4)
-        first_layer(2, 0, 0)
-        spread("s", 1)
-        second_layer(0)
-        first_layer(2, 0, 1)
-        relu("s", 3, 1)
-        take_y("v", 0)
-        first_layer(2, 0, 2)
-        quant_h(1)
-        turn(3, 0)
+        for s in range(PASSES):
+            for u in range(2):
+                round_x("scalar", s, u, 0, SPLIT)
+                round_x("vector", s, u, SPLIT, T)
+                if s > 0 and u == 0:
+                    interleave("scalar", "slot", s - 1, 0, S)
+                    quantise_x("token", s - 1, SPLIT, T)
+                if s > 0 and u == 1:
+                    quantise_x("slot", s - 1, 0, S)
+                    for kind, block in STREAMED:
+                        first_layer(kind, block, s - 1)
+                if u == 1:
+                    interleave("scalar", "token", s, SPLIT, T)
+                if (s, u) == (PASSES - 1, 1):
+                    for e in range(E):
+                        gather(s, u, C * e, C * (e + 1))
+                        interleave("scalar", "slot", s, C * e, C * (e + 1))
+                else:
+                    gather(s, u, 0, S)
+                if (s, u) == (1, 0):
+                    interleave("vector", "token", 0, 0, SPLIT)
+
+        last = PASSES - 1
+        quantise_x("token", last, SPLIT, T)
+        quantise_x("slot", last, 0, C)
+        for block in (4, 5):
+            first_layer("token", block, last)
+            relu("scalar", "token", block)
+        interleave("vector", "token", 2, 0, SPLIT)
+        quantise_x("slot", last, C, S)
+        quantise_x("token", 2, 0, SPLIT)
+        for block in (0, 1, 3):
+            first_layer("slot", block, last)
+        for s in range(last):
+            first_layer("slot", 2, s)
+        for block in (0, 1, 3):
+            relu("vector" if block == 3 else "scalar", "slot", block)
+        for b in range(2):
+            turn("token", 4 + b)
+            turn("slot", b)
+        spread("token", 2)
+        spread("slot", 0)
+        quantise_x("token", 0, 0, SPLIT)
+        first_layer("slot", 2, last)
+        interleave("vector", "token", 1, 0, SPLIT)
+        relu("vector", "slot", 2)
+        quantise_x("token", 1, 0, SPLIT)
+
+        for block in range(4):
+            first_layer("token", block, 0)
+        for block in (2, 3):
+            turn("slot", block)
+        quantise_h("slot", 0)
+        quantise_h("token", 2)
+        spread("slot", 1)
+        for block in (2, 3):
+            first_layer("token", block, 1)
+        second_layer("slot", 0)
+        take_y(0)
+        quantise_h("slot", 1)
         scatter(0)
-        relu("s", 2, 0)
-        turn(3, 1)
-        second_layer(1)
-        spread("s", 3)
-        take_y("s", 1)
-        quant_h(3)
-        turn(2, 0)
+        for block in (2, 3):
+            first_layer("token", block, 2)
+            relu("scalar", "token", block)
+        second_layer("slot", 1)
+        for block in (0, 1):
+            first_layer("token", block, 1)
+            first_layer("token", block, 2)
+        take_y(1)
         scatter(1)
-        turn(2, 1)
-        second_layer(3)
-        spread("s", 2)
-        take_y("s", 3)
-        quant_h(2)
+        second_layer("token", 2)
+
+        for block in (0, 1):
+            relu("scalar", "token", block)
+        for block in (2, 3, 0, 1):
+            turn("token", block)
+        spread("token", 1)
+        spread("token", 0)
+        quantise_h("token", 1)
         finish(2)
+        second_layer("token", 1)
+        quantise_h("token", 0)
         finish(1)
-        second_layer(2)
-        take_y("s", 2)
+        second_layer("token", 0)
         finish(0)

from contextlib import ExitStack

import concourse.mybir as mybir
from concourse.masks import make_identity

K, T, E, C, H, N = 1536, 768, 2, 256, 512, 128

P = 128
S = E * C
K_PASS = 512
PASSES = K // K_PASS
QUADRANTS = 4
SHARED = E
UNIT = 2 * P

FLOPS = 2 * (S + T) * (K * H + H * N)

F32 = mybir.dt.float32
BF16 = mybir.dt.bfloat16
I32 = mybir.dt.int32
U32 = mybir.dt.uint32
U16 = mybir.dt.uint16
U8 = mybir.dt.uint8
FP8X4 = mybir.dt.float8_e4m3fn_x4
FP4X4 = mybir.dt.float4_e2m1fn_x4

RELU = mybir.ActivationFunctionType.Relu
MULT = mybir.AluOpType.mult
ADD = mybir.AluOpType.add

SPLIT = 512

STREAMED = (("token", 4), ("token", 5), ("slot", 0), ("slot", 1), ("slot", 3))


def tile_moe_shr_mlp_relu_kernel(
    tc, xT, w1_words, w1_scales, w2_words, w2_scales, gate, offs, out
):
    nc = tc.nc
    with ExitStack() as ctx:
        keep = ctx.enter_context(tc.tile_pool(name="keep", bufs=1))
        psum = ctx.enter_context(tc.psum_pool(name="psum", bufs=1))

        offsets = keep.tile([P, S // 16], U16, name="offsets")
        gate_sb = keep.tile([P, S], F32, name="gate_sb")
        w2_codes = keep.tile([P, E + 1, 2 * N], U8, align_bytes=64, name="w2_codes")
        w1_planes = keep.tile([P, (E + 1) * PASSES, H], U8, align_bytes=64, name="w1_planes")
        w2_planes = keep.tile([P, E + 1, N], U8, align_bytes=64, name="w2_planes")
        ident = keep.tile([P, P], F32, name="ident")
        routed = keep.tile([P, T], F32, name="routed")
        routed_y = keep.tile([P, S], F32, name="routed_y")
        result = keep.tile([P, T], F32, name="result")

        x_raw, w1_codes, x_pairs, slot_pairs = {}, {}, {}, {}
        quads, codes, planes = {}, {}, {}
        for s in range(PASSES):
            x_raw[s] = keep.tile([P, 4, T], F32, name=f"x_raw{s}")
            w1_codes[s] = keep.tile([P, E + 1, 2 * H], U8, align_bytes=64, name=f"w1_codes{s}")
            x_pairs[s] = keep.tile([P, 2, T, 2], BF16, align_bytes=64, name=f"x_pairs{s}")
            slot_pairs[s] = keep.tile([P, 2, S, 2], BF16, align_bytes=64, name=f"slot_pairs{s}")
        h_rows, h_quads, h_codes, h_planes = {}, {}, {}, {}
        for kind, n in (("slot", S), ("token", T)):
            for s in range(PASSES):
                quads[kind, s] = keep.tile([P, n, 4], BF16, align_bytes=64, name=f"{kind}_quads{s}")
                codes[kind, s] = keep.tile([P, n], U32, align_bytes=64, name=f"{kind}_codes{s}")
                planes[kind, s] = keep.tile([P, n], U8, align_bytes=64, name=f"{kind}_planes{s}")
            h_rows[kind] = keep.tile([P, n // P, H], BF16, align_bytes=64, name=f"{kind}_h_rows")
            h_quads[kind] = keep.tile([P, n, 4], BF16, align_bytes=64, name=f"{kind}_h_quads")
            h_codes[kind] = keep.tile([P, n], U32, align_bytes=64, name=f"{kind}_h_codes")
            h_planes[kind] = keep.tile([P, n], U8, align_bytes=64, name=f"{kind}_h_planes")

        warm = keep.tile([P, 1], F32, name="warm")
        nc.vector.memset(warm[:], 0.0)
        nc.scalar.activation(warm[:], warm[:], RELU)

        w1_plane_words = w1_planes[:].rearrange("p a i -> p (a i)").bitcast(I32)
        w2_plane_words = w2_planes[:].rearrange("p a i -> p (a i)").bitcast(I32)
        half = (E + 1) * PASSES * H // 4 // 2
        nc.vector.memset(w1_plane_words[:, :half], 0)
        nc.gpsimd.memset(w1_plane_words[:, half:], 0)
        nc.gpsimd.memset(w2_plane_words, 0)

        def load_x(s, u, first, end):
            rows = xT[K_PASS * s : K_PASS * (s + 1), :].rearrange("(p d) t -> p d t", d=4)
            pair = slice(2 * u, 2 * u + 2)
            nc.sync.dma_start(x_raw[s][:, pair, first:end], rows[:, pair, first:end])

        def load_codes(tile, words):
            experts = E + 1
            nc.sync.dma_start(
                tile[:].rearrange("p e b -> p (e b)").bitcast(I32).rearrange("p (e b) -> p e b", e=experts),
                words.rearrange("e p b -> p e b"),
            )

        for first in range(0, T, UNIT):
            load_x(0, 0, first, first + UNIT)
        nc.sync.dma_start(offsets[:], offs)
        for q in range(QUADRANTS):
            nc.gpsimd.dma_start(
                w1_plane_words.rearrange("p (a i) -> p a i", i=H // 4)[32 * q : 32 * q + 4],
                w1_scales.bitcast(I32)[:, :, 4 * q : 4 * q + 4, :].rearrange("e s q i -> q (e s) i"),
            )
        load_x(0, 1, 0, T)
        load_x(1, 0, 0, T)
        load_x(1, 1, 0, T)
        load_x(2, 0, 0, T)
        load_codes(w1_codes[0], w1_words.bitcast(I32)[:, 0])
        load_x(2, 1, 0, T)
        load_codes(w1_codes[1], w1_words.bitcast(I32)[:, 1])
        load_codes(w1_codes[2], w1_words.bitcast(I32)[:, 2])
        load_codes(w2_codes, w2_words.bitcast(I32)[:, 0])
        nc.sync.dma_start(gate_sb[:], gate)
        for q in range(QUADRANTS):
            nc.sync.dma_start(
                w2_plane_words.rearrange("p (a i) -> p a i", i=N // 4)[32 * q : 32 * q + 4],
                w2_scales.bitcast(I32)[:, 0, 4 * q : 4 * q + 4, :].rearrange("e q i -> q e i"),
            )

        make_identity(nc, ident[:])
        nc.gpsimd.memset(routed[:], 0.0)

        def copy(engine, dst, src):
            if engine == "vector":
                nc.vector.tensor_copy(dst, src)
            else:
                nc.scalar.copy(dst, src)

        def as_words(tile, columns):
            return tile[:, columns].rearrange("p c d -> p (c d)").bitcast(F32).rearrange("p (c u) -> p c u", u=2)

        def round_x(engine, s, u, first, end):
            copy(
                engine,
                x_pairs[s][:, u, first:end, :],
                x_raw[s][:, 2 * u : 2 * u + 2, first:end].rearrange("p d t -> p t d"),
            )

        def gather(s, u, first, end):
            nc.vector.tensor_copy(
                slot_pairs[s][:, u, first:end].rearrange("p c d -> p (c d)").bitcast(U32),
                x_pairs[s][:, u].rearrange("p t d -> p (t d)").bitcast(U32).indirect(offsets[:, first // 16 : end // 16]),
            )

        def interleave(engine, kind, s, first, end):
            pairs = slot_pairs[s] if kind == "slot" else x_pairs[s]
            words = pairs[:].rearrange("p u c d -> p (u c d)").bitcast(F32).rearrange("p (u c) -> p c u", u=2)
            copy(engine, as_words(quads[kind, s], slice(first, end)), words[:, first:end])

        def quantise_x(kind, s, first, end):
            nc.vector.quantize_mx(
                out=codes[kind, s][:, first:end].bitcast(FP8X4),
                scales=planes[kind, s][:, first:end],
                in_=quads[kind, s][:, first:end].rearrange("p c d -> p (c d)"),
            )

        def expert_of(kind, block):
            return block * P // C if kind == "slot" else SHARED

        bank = {}

        def first_layer(kind, block, s):
            if s == 0:
                bank[kind, block] = psum.tile([P, H], F32, tag="sums", bufs=5, name="sums")
            e = expert_of(kind, block)
            columns = slice(P * block, P * (block + 1))
            nc.tensor.matmul_mx(
                out=bank[kind, block][:],
                lhsT=codes[kind, s][:, columns].bitcast(FP8X4),
                lhsT_scale=planes[kind, s][:, columns],
                rhs=w1_codes[s][:, e, :].bitcast(FP4X4),
                rhs_scale=w1_planes[:, e * PASSES + s, :],
                start=(s == 0),
                stop=(s == PASSES - 1),
            )

        def relu(engine, kind, block):
            if engine == "vector":
                nc.vector.tensor_scalar_max(h_rows[kind][:, block], bank[kind, block][:], 0.0)
            else:
                nc.scalar.activation(h_rows[kind][:, block], bank[kind, block][:], RELU)

        turned = {}

        def turn(kind, block):
            unit, b = divmod(block, 2)
            if b == 0:
                turned[kind, unit] = psum.tile([P, 2, 2, P], F32, tag="turned", bufs=2, name="turned")
            words = h_rows[kind][:, block].bitcast(F32)
            for u in range(2):
                nc.tensor.transpose(turned[kind, unit][:, b, u, :], words[:, u : H // 2 : 2], ident[:])

        def unit_columns(unit):
            return slice(UNIT * unit, UNIT * (unit + 1))

        def spread(kind, unit):
            nc.scalar.copy(
                as_words(h_quads[kind], unit_columns(unit)).rearrange("p (b c) u -> p b c u", b=2),
                turned[kind, unit][:].rearrange("p b u c -> p b c u"),
            )

        def quantise_h(kind, unit):
            columns = unit_columns(unit)
            nc.vector.quantize_mx(
                out=h_codes[kind][:, columns].bitcast(FP8X4),
                scales=h_planes[kind][:, columns],
                in_=h_quads[kind][:, columns].rearrange("p c d -> p (c d)"),
            )

        y = {}

        def second_layer(kind, unit):
            columns = unit_columns(unit)
            e = expert_of(kind, 2 * unit)
            if kind == "slot":
                y[kind, unit] = psum.tile([P, UNIT], F32, tag="y", bufs=1, name="y")
            else:
                y[kind, unit] = psum.tile([P, UNIT], F32, tag="sums", bufs=5, name="ys")
            nc.tensor.matmul_mx(
                out=y[kind, unit][:],
                lhsT=w2_codes[:, e, :].bitcast(FP4X4),
                lhsT_scale=w2_planes[:, e, :],
                rhs=h_codes[kind][:, columns].bitcast(FP8X4),
                rhs_scale=h_planes[kind][:, columns],
                start=True,
                stop=True,
            )

        def take_y(unit):
            nc.scalar.copy(routed_y[:, unit_columns(unit)], y["slot", unit][:])

        def scatter(unit):
            columns = unit_columns(unit)
            nc.vector.tensor_tensor(
                routed[:].indirect(offsets[:, UNIT // 16 * unit : UNIT // 16 * (unit + 1)]),
                routed_y[:, columns],
                gate_sb[:, columns],
                MULT,
            )

        def finish(unit):
            columns = unit_columns(unit)
            nc.vector.tensor_tensor(result[:, columns], y["token", unit][:], routed[:, columns], ADD)
            nc.sync.dma_start(out[:, columns], result[:, columns])

        for s in range(PASSES):
            for u in range(2):
                round_x("scalar", s, u, 0, SPLIT)
                round_x("vector", s, u, SPLIT, T)
                if s > 0 and u == 0:
                    interleave("scalar", "slot", s - 1, 0, S)
                    quantise_x("token", s - 1, SPLIT, T)
                if s > 0 and u == 1:
                    quantise_x("slot", s - 1, 0, S)
                    for kind, block in STREAMED:
                        first_layer(kind, block, s - 1)
                if u == 1:
                    interleave("scalar", "token", s, SPLIT, T)
                if (s, u) == (PASSES - 1, 1):
                    for e in range(E):
                        gather(s, u, C * e, C * (e + 1))
                        interleave("scalar", "slot", s, C * e, C * (e + 1))
                else:
                    gather(s, u, 0, S)
                if (s, u) == (1, 0):
                    interleave("vector", "token", 0, 0, SPLIT)

        last = PASSES - 1
        quantise_x("token", last, SPLIT, T)
        quantise_x("slot", last, 0, C)
        for block in (4, 5):
            first_layer("token", block, last)
            relu("scalar", "token", block)
        interleave("vector", "token", 2, 0, SPLIT)
        quantise_x("slot", last, C, S)
        quantise_x("token", 2, 0, SPLIT)
        for block in (0, 1, 3):
            first_layer("slot", block, last)
        for s in range(last):
            first_layer("slot", 2, s)
        for block in (0, 1, 3):
            relu("vector" if block == 3 else "scalar", "slot", block)
        for b in range(2):
            turn("token", 4 + b)
            turn("slot", b)
        spread("token", 2)
        spread("slot", 0)
        quantise_x("token", 0, 0, SPLIT)
        first_layer("slot", 2, last)
        interleave("vector", "token", 1, 0, SPLIT)
        relu("vector", "slot", 2)
        quantise_x("token", 1, 0, SPLIT)

        for block in range(4):
            first_layer("token", block, 0)
        for block in (2, 3):
            turn("slot", block)
        quantise_h("slot", 0)
        quantise_h("token", 2)
        spread("slot", 1)
        for block in (2, 3):
            first_layer("token", block, 1)
        second_layer("slot", 0)
        take_y(0)
        quantise_h("slot", 1)
        scatter(0)
        for block in (2, 3):
            first_layer("token", block, 2)
            relu("scalar", "token", block)
        second_layer("slot", 1)
        for block in (0, 1):
            first_layer("token", block, 1)
            first_layer("token", block, 2)
        take_y(1)
        scatter(1)
        second_layer("token", 2)

        for block in (0, 1):
            relu("scalar", "token", block)
        for block in (2, 3, 0, 1):
            turn("token", block)
        spread("token", 1)
        spread("token", 0)
        quantise_h("token", 1)
        finish(2)
        second_layer("token", 1)
        quantise_h("token", 0)
        finish(1)
        second_layer("token", 0)
        finish(0)
